import numpy as np
import ml_dtypes


def mxq(x, axis, fmt="e4m3"):
    dtype, down = {"e4m3": (ml_dtypes.float8_e4m3fn, 7), "e5m2": (ml_dtypes.float8_e5m2, 14)}[fmt]
    v = np.moveaxis(np.asarray(x, np.float32).astype(ml_dtypes.bfloat16).astype(np.float64), axis, -1)
    blocks = v.reshape(v.shape[:-1] + (-1, 32))
    amax = np.abs(blocks).max(-1, keepdims=True)
    byte = np.maximum(np.where(amax > 0, np.frexp(amax)[1] - 1 + 127, 0) - down, 1)
    scale = np.exp2(byte - 127.0)
    codes = (blocks / scale).astype(np.float32).astype(dtype).astype(np.float64)
    return np.moveaxis((codes * scale).reshape(v.shape), -1, axis)


WIDE = False


def mx_kscale(k):
    if not WIDE:
        return np.ones(k)
    levels = np.array([10, -10, 5, -5, 0])
    if k % 512:
        return np.exp2(np.random.permutation(np.resize(levels, k // 32))).repeat(32)
    a = np.empty((k // 512, 16))
    for p in range(k // 512):
        a[p, :8] = np.random.permutation(np.resize(levels, 8))
        for g in range(8):
            far = levels[np.abs(levels - a[p, g]) >= 10]
            a[p, g + 8] = far[np.random.randint(len(far))]
    return np.exp2(a.ravel()).repeat(32)


def f64(x):
    return np.asarray(x).astype(np.float64)


def striped(idx):
    return np.tile(idx.reshape(-1, 16).T, (8, 1)).astype(np.uint16)


def unstriped(offs):
    return offs[:16].T.reshape(-1).astype(np.int64)


E2M1 = np.array([0.0, 0.5, 1.0, 1.5, 2.0, 3.0, 4.0, 6.0, -0.0, -0.5, -1.0, -1.5, -2.0, -3.0, -4.0, -6.0])


def pack_weight(w, fmt):
    k, n = w.shape
    w = f64(np.asarray(w, np.float32).astype(ml_dtypes.bfloat16)).reshape(k // 32, 32, n)
    amax = np.abs(w).max(1)
    if fmt == "e4m3":
        byte = np.frexp(amax)[1] - 1 + 127 - 7
    else:
        mant, ex = np.frexp(amax / 6.0)
        byte = np.where(mant > 0.5, ex, ex - 1) + 127
    byte = np.clip(np.where(amax > 0, byte, 1), 1, 254)
    scaled = (w * np.exp2(127.0 - byte)[:, None, :]).reshape(k, n).astype(np.float32)
    by_word = np.ascontiguousarray(scaled.reshape(k // 512, 128, 4, n).transpose(0, 1, 3, 2))
    if fmt == "e4m3":
        words = by_word.astype(ml_dtypes.float8_e4m3fn).view(np.uint8)
    else:
        c = by_word.astype(ml_dtypes.float4_e2m1fn).view(np.uint8) & 0xF
        words = (c[..., 0::2] | (c[..., 1::2] << 4)).reshape(k // 512, 128, 2 * n)
    return np.ascontiguousarray(words), np.ascontiguousarray(byte.astype(np.uint8).reshape(k // 512, 16, n))


def unpack_weight(words, scales, fmt):
    g, _, n = scales.shape
    words = np.ascontiguousarray(words).reshape(g, 128, n, -1)
    if fmt == "e4m3":
        vals = words.view(ml_dtypes.float8_e4m3fn).astype(np.float64)
    else:
        nib = np.empty((g, 128, n, 4), np.uint8)
        nib[..., 0::2] = words & 0xF
        nib[..., 1::2] = words >> 4
        vals = E2M1[nib]
    vals = vals * np.repeat(np.exp2(scales.astype(np.float64) - 127.0), 8, axis=1)[..., None]
    return vals.transpose(0, 1, 3, 2).reshape(g * 512, n)


def gelu(v):
    return 0.5 * v * (1.0 + np.tanh(np.sqrt(2.0 / np.pi) * (v + 0.044715 * v**3)))


K, H, T, S, T3, S2, P = 1024, 1024, 4096, 1024, 2048, 512, 512

def setup_inputs():
    n = np.random.standard_normal
    s = mx_kscale(K)[:, None]
    u = mx_kscale(H)[:, None]
    d = {}
    d["tab_words"], d["tab_scales"] = pack_weight(n((K, T)) * s, "e4m3")
    d["offs"] = striped(np.random.permutation(T)[:S])
    d["w1"] = (n((K, H)) / K ** 0.5 / s * u.T).astype(np.float32)
    d["w4_words"], d["w4_scales"] = pack_weight(n((K, H)) / K ** 0.5 / s * u.T, "e2m1")
    d["gam"] = (np.exp(0.3 * n(H)) / u[:, 0]).astype(np.float32)
    d["tab2_words"], d["tab2_scales"] = pack_weight(0.7 * n((H, T3)) / H ** 0.5 / u, "e4m3")
    d["offs2"] = striped(np.random.permutation(T3)[:S2])
    d["pos1"] = striped(np.random.permutation(S)[:P])
    d["pos2"] = striped(np.random.permutation(S)[:P])
    d["typ"] = n((S2, P)).astype(np.float32)
    return d

def reference(tab_words, tab_scales, offs, w1, w4_words, w4_scales, gam, tab2_words, tab2_scales, offs2, pos1, pos2, typ):
    v = unpack_weight(tab_words, tab_scales, "e4m3")[:, unstriped(offs)]
    v2 = unpack_weight(tab2_words, tab2_scales, "e4m3")[:, unstriped(offs2)]
    w4 = unpack_weight(w4_words, w4_scales, "e2m1")
    x = mxq(f64(w1), 0, "e4m3").T @ v
    y = w4.T @ v
    h = np.abs(x - y) + f64(gam)[:, None] * x * y
    e = v2.T @ mxq(h, 0, "e4m3")
    return e[:, unstriped(pos1)] * e[:, unstriped(pos2)] - f64(typ)

@@ -1,0 +1,258 @@
+from contextlib import ExitStack
+
+import concourse.mybir as mybir
+
+K, H, T, S, T3, S2, NP = 1024, 1024, 4096, 1024, 2048, 512, 512
+FLOPS = 2 * (2 * K * H * S + H * S2 * S)
+
+F32 = mybir.dt.float32
+BF16 = mybir.dt.bfloat16
+I32 = mybir.dt.int32
+U32 = mybir.dt.uint32
+U16 = mybir.dt.uint16
+U8 = mybir.dt.uint8
+FP8X4 = mybir.dt.float8_e4m3fn_x4
+FP4X4 = mybir.dt.float4_e2m1fn_x4
+ALU = mybir.AluOpType
+ACT = mybir.ActivationFunctionType
+
+P = 128
+PACK = 4
+PASS = P * PACK
+N = 512
+LIST_COLS = N // 16
+
+
+def tile_list_excerpt_pair_scores_kernel(
+    tc, tab_words, tab_scales, offs, w1, w4_words, w4_scales, gam, tab2_words, tab2_scales, offs2, pos1, pos2, typ, out
+):
+    nc = tc.nc
+    with ExitStack() as ctx:
+        keep = ctx.enter_context(tc.tile_pool(name="keep", bufs=1))
+        ring = ctx.enter_context(tc.tile_pool(name="ring", bufs=2))
+        psum = ctx.enter_context(tc.psum_pool(name="psum", bufs=1))
+
+        def held(name, shape, dtype):
+            return keep.tile(shape, dtype, name=name, align_bytes=64)
+
+        idx = held("idx", [P, S // 16], U16)
+        idx2 = held("idx2", [P, S2 // 16], U16)
+        p1 = held("p1", [P, NP // 16], U16)
+        p2 = held("p2", [P, NP // 16], U16)
+
+        tab_sc = held("tab_sc", [P, T], U8)
+        tab2_sc = held("tab2_sc", [P, T3], U8)
+        w4_sc_raw = held("w4_sc_raw", [P, 2 * H], U8)
+        v_planes = [held(f"v_plane{a}", [P, S], U8) for a in range(2)]
+        w4_sc = held("w4_sc", [P, 4 * PASS], U8)
+        for q in range(4):
+            nc.vector.memset(tab_sc[32 * q : 32 * q + 24, :].bitcast(I32), 0)
+        for q in range(4):
+            nc.vector.memset(w4_sc_raw[32 * q : 32 * q + 28, :].bitcast(I32), 0)
+        for plane in (v_planes[0], v_planes[1], w4_sc, tab2_sc):
+            nc.gpsimd.memset(plane[:].bitcast(I32), 0)
+
+        tab_w = [held(f"tab_w{a}", [P, T], I32) for a in range(2)]
+        tab2_w = [held(f"tab2_w{a}", [P, T3], I32) for a in range(2)]
+        w4_raw = held("w4_raw", [P, 2, 2 * H], U8)
+        w1_raw = {(a, b): held(f"w1_raw{a}{b}", [P, PACK, PASS], F32) for a in range(2) for b in range(2)}
+        gain = held("gain", [P, 2, PACK], F32)
+        typ_sb = held("typ_sb", [P, S2 // P, NP], F32)
+
+        def load_scale_rows(window, scales, row):
+            for q in range(4):
+                nc.sync.dma_start(
+                    out=window[32 * q + row : 32 * q + row + 8, :].bitcast(I32),
+                    in_=scales[:, 4 * q : 4 * q + 4, :].bitcast(I32),
+                )
+
+        def lift_rows(plane, source, row):
+            nc.gpsimd.dma_start(out=plane[0 : P - row, :].bitcast(I32), in_=source[row:P, :].bitcast(I32))
+
+        def load_words(window, words):
+            nc.sync.dma_start(out=window[:], in_=words.rearrange("p t i -> p (t i)").bitcast(I32))
+
+        def load_w1(a, b):
+            rows = w1[PASS * a : PASS * (a + 1), PASS * b : PASS * (b + 1)]
+            nc.sync.dma_start(out=w1_raw[a, b][:], in_=rows.rearrange("(p j) c -> p j c", j=PACK))
+
+        nc.sync.dma_start(idx[:], offs)
+        load_scale_rows(tab_sc, tab_scales, 24)
+        nc.sync.dma_start(out=w4_raw[:].bitcast(I32), in_=w4_words.rearrange("a p c -> p a c").bitcast(I32))
+        load_w1(0, 0)
+        load_w1(1, 0)
+        for q in range(4):
+            nc.sync.dma_start(
+                out=w4_sc_raw[32 * q + 28 : 32 * q + 32, :].bitcast(I32).rearrange("r (a c) -> r a c", a=2),
+                in_=w4_scales[:, 4 * q : 4 * q + 4, :].bitcast(I32).rearrange("a r c -> r a c"),
+            )
+        load_words(tab_w[0], tab_words[0])
+        load_words(tab_w[1], tab_words[1])
+        nc.sync.dma_start(out=gain[:], in_=gam.rearrange("(b p t) -> p b t", b=2, t=PACK))
+        nc.sync.dma_start(idx2[:], offs2)
+        load_scale_rows(tab2_sc, tab2_scales, 0)
+        load_w1(0, 1)
+        load_words(tab2_w[0], tab2_words[0])
+        load_w1(1, 1)
+        load_words(tab2_w[1], tab2_words[1])
+        nc.sync.dma_start(p1[:], pos1)
+        nc.sync.dma_start(p2[:], pos2)
+        nc.sync.dma_start(out=typ_sb[:], in_=typ.rearrange("(g p) n -> p g n", p=P))
+
+        v_sc = held("v_sc", [P, S], U8)
+        nc.vector.tensor_copy(v_sc[:], tab_sc[:].indirect(idx[:]))
+        for a in range(2):
+            lift_rows(v_planes[a], v_sc, 24 + 4 * a)
+
+        w4_c = held("w4_c", [P, 4 * 2 * PASS], U8)
+        w4_sc_dealt = held("w4_sc_dealt", [P, 4 * PASS], U8)
+        nc.vector.tensor_copy(
+            out=w4_c[:].bitcast(U16).rearrange("p (g t q) -> p g t q", g=4, t=PACK),
+            in_=w4_raw[:].rearrange("p a c -> p (a c)").bitcast(U16).rearrange("p (g q t) -> p g t q", g=4, t=PACK),
+        )
+        nc.vector.tensor_copy(
+            out=w4_sc_dealt[:].rearrange("p (g t q) -> p g t q", g=4, t=PACK),
+            in_=w4_sc_raw[:].rearrange("p (g q t) -> p g t q", g=4, t=PACK),
+        )
+        lift_rows(w4_sc, w4_sc_dealt, 28)
+
+        w1_bf = {}
+        w1_c = {(a, b): held(f"w1_c{a}{b}", [P, PASS], U32) for a in range(2) for b in range(2)}
+        w1_sc = {(a, b): held(f"w1_sc{a}{b}", [P, PASS], U8) for a in range(2) for b in range(2)}
+
+        def round_w1(a, b, q0, q1):
+            if q0 == 0:
+                w1_bf[a, b] = held(f"w1_bf{a}", [P, PACK * PASS], BF16)
+            nc.scalar.copy(
+                out=w1_bf[a, b][:].rearrange("p (t q j) -> p q j t", t=PACK, j=PACK)[:, q0:q1],
+                in_=w1_raw[a, b][:].rearrange("p j (q t) -> p q j t", t=PACK)[:, q0:q1],
+            )
+
+        def quantise_w1(a, b):
+            nc.vector.quantize_mx(out=w1_c[a, b][:].bitcast(FP8X4), scales=w1_sc[a, b][:], in_=w1_bf[a, b][:])
+
+        for a in range(2):
+            round_w1(a, 0, 0, P)
+            quantise_w1(a, 0)
+
+        v_w = {(a, half): held(f"v_w{a}{half}", [P, N], U32) for a in range(2) for half in range(2)}
+        for a in range(2):
+            for half in range(2):
+                picks = idx[:, LIST_COLS * half : LIST_COLS * (half + 1)]
+                nc.vector.tensor_copy(v_w[a, half][:], tab_w[a][:].bitcast(U32).indirect(picks))
+
+        v2_sc = held("v2_sc", [P, S2], U8)
+        nc.vector.tensor_copy(v2_sc[:], tab2_sc[:].indirect(idx2[:]))
+        v2_w = [held(f"v2_w{b}", [P, S2], U32) for b in range(2)]
+
+        def gather_v2(b):
+            nc.vector.tensor_copy(v2_w[b][:], tab2_w[b][:].bitcast(U32).indirect(idx2[:]))
+
+        h_c = {(b, half): held(f"h_c{b}{half}", [P, N], U32) for b in range(2) for half in range(2)}
+        h_sc = {(b, half): held(f"h_sc{b}{half}", [P, N], U8) for b in range(2) for half in range(2)}
+        scores = [held(f"scores{g}", [P, S], F32) for g in range(S2 // P)]
+
+        def readings(b, half, t, apart, joint):
+            x_ps = psum.tile([P, N], F32, name="x_ps", bufs=2)
+            y_ps = psum.tile([P, N], F32, name="y_ps", bufs=2)
+            cols = slice(N * half, N * (half + 1))
+            for a in range(2):
+                nc.tensor.matmul_mx(
+                    out=x_ps[:],
+                    lhsT=w1_c[a, b][:, P * t : P * (t + 1)].bitcast(FP8X4),
+                    lhsT_scale=w1_sc[a, b][:, P * t : P * (t + 1)],
+                    rhs=v_w[a, half][:].bitcast(FP8X4),
+                    rhs_scale=v_planes[a][:, cols],
+                    start=(a == 0),
+                    stop=(a == 1),
+                )
+            for a in range(2):
+                first = PASS * (2 * a + b) + P * t
+                nc.tensor.matmul_mx(
+                    out=y_ps[:],
+                    lhsT=w4_c[:, 2 * first : 2 * (first + P)].bitcast(FP4X4),
+                    lhsT_scale=w4_sc[:, first : first + P],
+                    rhs=v_w[a, half][:].bitcast(FP8X4),
+                    rhs_scale=v_planes[a][:, cols],
+                    start=(a == 0),
+                    stop=(a == 1),
+                )
+            x_sb = ring.tile([P, N], F32, name="x_sb", bufs=3)
+            diff = ring.tile([P, N], F32, name="diff", bufs=3)
+            nc.scalar.copy(out=x_sb[:], in_=x_ps[:])
+            nc.vector.tensor_tensor(out=diff[:], in0=y_ps[:], in1=x_sb[:], op=ALU.subtract)
+            nc.vector.scalar_tensor_tensor(
+                out=joint[:, t, :], in0=y_ps[:], scalar=gain[:, b, t : t + 1], in1=x_sb[:], op0=ALU.mult, op1=ALU.mult
+            )
+            nc.scalar.activation(out=apart[:, t, :], in_=diff[:], func=ACT.Abs)
+
+        def join(h_bf, apart, joint, c0, c1):
+            nc.vector.tensor_tensor(
+                out=h_bf[:].rearrange("p (c i t) -> p c t i", i=4, t=PACK)[:, c0:c1],
+                in0=apart[:].rearrange("p t (c i) -> p c t i", i=4)[:, c0:c1],
+                in1=joint[:].rearrange("p t (c i) -> p c t i", i=4)[:, c0:c1],
+                op=ALU.add,
+            )
+
+        def quantise_h(chunk, h_bf):
+            nc.vector.quantize_mx(out=h_c[chunk][:].bitcast(FP8X4), scales=h_sc[chunk][:], in_=h_bf[:])
+
+        def score_pass(bank, g, b, half):
+            nc.tensor.matmul_mx(
+                out=bank[:],
+                lhsT=v2_w[b][:, P * g : P * (g + 1)].bitcast(FP8X4),
+                lhsT_scale=v2_sc[4 * b : P, P * g : P * (g + 1)],
+                rhs=h_c[b, half][:].bitcast(FP8X4),
+                rhs_scale=h_sc[b, half][:],
+                start=(b == 0),
+                stop=(b == 1),
+            )
+
+        def score(half):
+            banks = [psum.tile([P, N], F32, name=f"e_ps{g}") for g in range(S2 // P)]
+            for b in range(2):
+                for g, bank in enumerate(banks):
+                    score_pass(bank, g, b, half)
+            for g, bank in enumerate(banks):
+                nc.scalar.copy(out=scores[g][:, N * half : N * (half + 1)], in_=bank[:])
+
+        chunks = [(b, half) for b in range(2) for half in range(2)]
+        quarter = N // 4 // PACK
+        behind = None
+        for n, (b, half) in enumerate(chunks):
+            apart = ring.tile([P, PACK, N], F32, name="apart")
+            joint = ring.tile([P, PACK, N], F32, name="joint")
+            for t in range(PACK):
+                readings(b, half, t, apart, joint)
+                if b == 0:
+                    round_w1(half, 1, 32 * t, 32 * (t + 1))
+                if behind is not None:
+                    join(*behind[1:], quarter * t, quarter * (t + 1))
+            if b == 0:
+                gather_v2(half)
+                quantise_w1(half, 1)
+            if behind is not None:
+                quantise_h(behind[0], behind[1])
+                if behind[0] == (1, 0):
+                    score(0)
+            h_bf = ring.tile([P, PACK * N], BF16, name="h_bf", align_bytes=64)
+            behind = ((b, half), h_bf, apart, joint)
+        join(*behind[1:], 0, 4 * quarter)
+        quantise_h(behind[0], behind[1])
+        score(1)
+
+        firsts, pairs = {}, {}
+        groups = S2 // P
+        for step in range(groups + 2):
+            if step < groups:
+                firsts[step] = ring.tile([P, NP], F32, name="first", bufs=2)
+                nc.vector.tensor_copy(firsts[step][:], scores[step][:].indirect(p1[:]))
+            g = step - 1
+            if 0 <= g < groups:
+                pairs[g] = ring.tile([P, NP], F32, name="pair", bufs=2)
+                nc.vector.tensor_tensor(pairs[g][:], scores[g][:].indirect(p2[:]), firsts[g][:], ALU.mult)
+            g = step - 2
+            if g >= 0:
+                result = ring.tile([P, NP], F32, name="result", bufs=3)
+                nc.vector.tensor_tensor(out=result[:], in0=pairs[g][:], in1=typ_sb[:, g, :], op=ALU.subtract)
+                nc.sync.dma_start(out=out[P * g : P * (g + 1), :], in_=result[:])

@@ -43,78 +43,55 @@ def tile_list_excerpt_pair_scores_kernel(
         tab_sc = held("tab_sc", [P, T], U8)
         tab2_sc = held("tab2_sc", [P, T3], U8)
         w4_sc_raw = held("w4_sc_raw", [P, 2 * H], U8)
-        v_planes = [held(f"v_plane{a}", [P, S], U8) for a in range(2)]
-        w4_sc = held("w4_sc", [P, 4 * PASS], U8)
-        for q in range(4):
-            nc.vector.memset(tab_sc[32 * q : 32 * q + 24, :].bitcast(I32), 0)
-        for q in range(4):
-            nc.vector.memset(w4_sc_raw[32 * q : 32 * q + 28, :].bitcast(I32), 0)
-        for plane in (v_planes[0], v_planes[1], w4_sc, tab2_sc):
-            nc.gpsimd.memset(plane[:].bitcast(I32), 0)
+        for plane in (tab_sc, w4_sc_raw, tab2_sc):
+            nc.vector.memset(plane[:].bitcast(I32), 0)
 
         tab_w = [held(f"tab_w{a}", [P, T], I32) for a in range(2)]
         tab2_w = [held(f"tab2_w{a}", [P, T3], I32) for a in range(2)]
         w4_raw = held("w4_raw", [P, 2, 2 * H], U8)
-        w1_raw = {(a, b): held(f"w1_raw{a}{b}", [P, PACK, PASS], F32) for a in range(2) for b in range(2)}
+        w1_raw = {}
         gain = held("gain", [P, 2, PACK], F32)
-        typ_sb = held("typ_sb", [P, S2 // P, NP], F32)
 
-        def load_scale_rows(window, scales, row):
+        def load_scale_rows(window, scales):
             for q in range(4):
                 nc.sync.dma_start(
-                    out=window[32 * q + row : 32 * q + row + 8, :].bitcast(I32),
-                    in_=scales[:, 4 * q : 4 * q + 4, :].bitcast(I32),
+                    out=window[32 * q : 32 * q + 8, :].bitcast(I32), in_=scales[:, 4 * q : 4 * q + 4, :].bitcast(I32)
                 )
-
-        def lift_rows(plane, source, row):
-            nc.gpsimd.dma_start(out=plane[0 : P - row, :].bitcast(I32), in_=source[row:P, :].bitcast(I32))
 
         def load_words(window, words):
             nc.sync.dma_start(out=window[:], in_=words.rearrange("p t i -> p (t i)").bitcast(I32))
 
         def load_w1(a, b):
+            w1_raw[a, b] = held(f"w1_raw{a}{b}", [P, PACK, PASS], F32)
             rows = w1[PASS * a : PASS * (a + 1), PASS * b : PASS * (b + 1)]
             nc.sync.dma_start(out=w1_raw[a, b][:], in_=rows.rearrange("(p j) c -> p j c", j=PACK))
 
-        nc.sync.dma_start(idx[:], offs)
-        load_scale_rows(tab_sc, tab_scales, 24)
+        for tile, entries in ((idx, offs), (idx2, offs2), (p1, pos1), (p2, pos2)):
+            nc.sync.dma_start(tile[:], entries)
+        nc.sync.dma_start(out=gain[:], in_=gam.rearrange("(b p t) -> p b t", b=2, t=PACK))
         nc.sync.dma_start(out=w4_raw[:].bitcast(I32), in_=w4_words.rearrange("a p c -> p a c").bitcast(I32))
         load_w1(0, 0)
         load_w1(1, 0)
+        load_scale_rows(tab_sc, tab_scales)
+        load_words(tab_w[0], tab_words[0])
         for q in range(4):
             nc.sync.dma_start(
-                out=w4_sc_raw[32 * q + 28 : 32 * q + 32, :].bitcast(I32).rearrange("r (a c) -> r a c", a=2),
+                out=w4_sc_raw[32 * q : 32 * q + 4, :].bitcast(I32).rearrange("r (a c) -> r a c", a=2),
                 in_=w4_scales[:, 4 * q : 4 * q + 4, :].bitcast(I32).rearrange("a r c -> r a c"),
             )
-        load_words(tab_w[0], tab_words[0])
         load_words(tab_w[1], tab_words[1])
-        nc.sync.dma_start(out=gain[:], in_=gam.rearrange("(b p t) -> p b t", b=2, t=PACK))
-        nc.sync.dma_start(idx2[:], offs2)
-        load_scale_rows(tab2_sc, tab2_scales, 0)
-        load_w1(0, 1)
-        load_words(tab2_w[0], tab2_words[0])
-        load_w1(1, 1)
-        load_words(tab2_w[1], tab2_words[1])
-        nc.sync.dma_start(p1[:], pos1)
-        nc.sync.dma_start(p2[:], pos2)
-        nc.sync.dma_start(out=typ_sb[:], in_=typ.rearrange("(g p) n -> p g n", p=P))
-
-        v_sc = held("v_sc", [P, S], U8)
-        nc.vector.tensor_copy(v_sc[:], tab_sc[:].indirect(idx[:]))
-        for a in range(2):
-            lift_rows(v_planes[a], v_sc, 24 + 4 * a)
+        load_scale_rows(tab2_sc, tab2_scales)
 
         w4_c = held("w4_c", [P, 4 * 2 * PASS], U8)
-        w4_sc_dealt = held("w4_sc_dealt", [P, 4 * PASS], U8)
         nc.vector.tensor_copy(
             out=w4_c[:].bitcast(U16).rearrange("p (g t q) -> p g t q", g=4, t=PACK),
             in_=w4_raw[:].rearrange("p a c -> p (a c)").bitcast(U16).rearrange("p (g q t) -> p g t q", g=4, t=PACK),
         )
-        nc.vector.tensor_copy(
-            out=w4_sc_dealt[:].rearrange("p (g t q) -> p g t q", g=4, t=PACK),
-            in_=w4_sc_raw[:].rearrange("p (g q t) -> p g t q", g=4, t=PACK),
-        )
-        lift_rows(w4_sc, w4_sc_dealt, 28)
+
+        v_sc = held("v_sc", [P, S], U8)
+        v_sc1 = held("v_sc1", [P, S], U8)
+        nc.vector.tensor_copy(v_sc[:], tab_sc[:].indirect(idx[:]))
+        v_planes = [v_sc, v_sc1]
 
         w1_bf = {}
         w1_c = {(a, b): held(f"w1_c{a}{b}", [P, PASS], U32) for a in range(2) for b in range(2)}
@@ -134,12 +111,26 @@ def tile_list_excerpt_pair_scores_kernel(
         for a in range(2):
             round_w1(a, 0, 0, P)
             quantise_w1(a, 0)
+        nc.scalar.dma_start(out=v_sc1[0 : P - 4, :].bitcast(I32), in_=v_sc[4:P, :].bitcast(I32))
 
+        load_w1(0, 1)
+        load_words(tab2_w[0], tab2_words[0])
+        load_words(tab2_w[1], tab2_words[1])
+        load_w1(1, 1)
+        typ_sb = held("w1_raw00", [P, S2 // P, NP], F32)
+        nc.sync.dma_start(out=typ_sb[:], in_=typ.rearrange("(g p) n -> p g n", p=P))
+
+        w4_sc = held("w4_sc", [P, 4 * PASS], U8)
         v_w = {(a, half): held(f"v_w{a}{half}", [P, N], U32) for a in range(2) for half in range(2)}
         for a in range(2):
             for half in range(2):
                 picks = idx[:, LIST_COLS * half : LIST_COLS * (half + 1)]
                 nc.vector.tensor_copy(v_w[a, half][:], tab_w[a][:].bitcast(U32).indirect(picks))
+            if a == 0:
+                nc.vector.tensor_copy(
+                    out=w4_sc[:].rearrange("p (g t q) -> p g t q", g=4, t=PACK),
+                    in_=w4_sc_raw[:].rearrange("p (g q t) -> p g t q", g=4, t=PACK),
+                )
 
         v2_sc = held("v2_sc", [P, S2], U8)
         nc.vector.tensor_copy(v2_sc[:], tab2_sc[:].indirect(idx2[:]))
@@ -150,11 +141,10 @@ def tile_list_excerpt_pair_scores_kernel(
 
         h_c = {(b, half): held(f"h_c{b}{half}", [P, N], U32) for b in range(2) for half in range(2)}
         h_sc = {(b, half): held(f"h_sc{b}{half}", [P, N], U8) for b in range(2) for half in range(2)}
-        scores = [held(f"scores{g}", [P, S], F32) for g in range(S2 // P)]
 
         def readings(b, half, t, apart, joint):
-            x_ps = psum.tile([P, N], F32, name="x_ps", bufs=2)
-            y_ps = psum.tile([P, N], F32, name="y_ps", bufs=2)
+            x_ps = psum.tile([P, N], F32, name="x_ps", bufs=4)
+            y_ps = psum.tile([P, N], F32, name="y_ps", bufs=4)
             cols = slice(N * half, N * (half + 1))
             for a in range(2):
                 nc.tensor.matmul_mx(
@@ -177,7 +167,7 @@ def tile_list_excerpt_pair_scores_kernel(
                     start=(a == 0),
                     stop=(a == 1),
                 )
-            x_sb = ring.tile([P, N], F32, name="x_sb", bufs=3)
+            x_sb = ring.tile([P, N], F32, name="x_sb", bufs=4)
             diff = ring.tile([P, N], F32, name="diff", bufs=3)
             nc.scalar.copy(out=x_sb[:], in_=x_ps[:])
             nc.vector.tensor_tensor(out=diff[:], in0=y_ps[:], in1=x_sb[:], op=ALU.subtract)
@@ -186,38 +176,45 @@ def tile_list_excerpt_pair_scores_kernel(
             )
             nc.scalar.activation(out=apart[:, t, :], in_=diff[:], func=ACT.Abs)
 
-        def join(h_bf, apart, joint, c0, c1):
+        def join(h_bf, apart, joint, part):
+            pairs = slice(part * N // 4, (part + 1) * N // 4)
             nc.vector.tensor_tensor(
-                out=h_bf[:].rearrange("p (c i t) -> p c t i", i=4, t=PACK)[:, c0:c1],
-                in0=apart[:].rearrange("p t (c i) -> p c t i", i=4)[:, c0:c1],
-                in1=joint[:].rearrange("p t (c i) -> p c t i", i=4)[:, c0:c1],
+                out=h_bf[:].rearrange("p (c i t) -> p c t i", i=2, t=PACK)[:, pairs],
+                in0=apart[:].rearrange("p t (c i) -> p c t i", i=2)[:, pairs],
+                in1=joint[:].rearrange("p t (c i) -> p c t i", i=2)[:, pairs],
                 op=ALU.add,
             )
 
-        def quantise_h(chunk, h_bf):
-            nc.vector.quantize_mx(out=h_c[chunk][:].bitcast(FP8X4), scales=h_sc[chunk][:], in_=h_bf[:])
-
-        def score_pass(bank, g, b, half):
-            nc.tensor.matmul_mx(
-                out=bank[:],
-                lhsT=v2_w[b][:, P * g : P * (g + 1)].bitcast(FP8X4),
-                lhsT_scale=v2_sc[4 * b : P, P * g : P * (g + 1)],
-                rhs=h_c[b, half][:].bitcast(FP8X4),
-                rhs_scale=h_sc[b, half][:],
-                start=(b == 0),
-                stop=(b == 1),
+        def quantise_h(chunk, h_bf, cols):
+            nc.vector.quantize_mx(
+                out=h_c[chunk][:, cols].bitcast(FP8X4),
+                scales=h_sc[chunk][:, cols],
+                in_=h_bf[:, PACK * cols.start : PACK * cols.stop],
             )
 
-        def score(half):
-            banks = [psum.tile([P, N], F32, name=f"e_ps{g}") for g in range(S2 // P)]
-            for b in range(2):
+        def score_pass(bank, g, b, half, cols, start, stop):
+            nc.tensor.matmul_mx(
+                out=bank[:, cols],
+                lhsT=v2_w[b][:, P * g : P * (g + 1)].bitcast(FP8X4),
+                lhsT_scale=v2_sc[4 * b : P, P * g : P * (g + 1)],
+                rhs=h_c[b, half][:, cols].bitcast(FP8X4),
+                rhs_scale=h_sc[b, half][:, cols],
+                start=start,
+                stop=stop,
+            )
+
+        def score(half, scores, banks, last_parts):
+            for g, bank in enumerate(banks):
+                score_pass(bank, g, 0, half, slice(0, N), True, False)
+            for cols in last_parts:
                 for g, bank in enumerate(banks):
-                    score_pass(bank, g, b, half)
+                    score_pass(bank, g, 1, half, cols, False, cols.stop == N)
             for g, bank in enumerate(banks):
                 nc.scalar.copy(out=scores[g][:, N * half : N * (half + 1)], in_=bank[:])
 
         chunks = [(b, half) for b in range(2) for half in range(2)]
-        quarter = N // 4 // PACK
+        whole = slice(0, N)
+        halves = [slice(0, N // 2), slice(N // 2, N)]
         behind = None
         for n, (b, half) in enumerate(chunks):
             apart = ring.tile([P, PACK, N], F32, name="apart")
@@ -226,33 +223,36 @@ def tile_list_excerpt_pair_scores_kernel(
                 readings(b, half, t, apart, joint)
                 if b == 0:
                     round_w1(half, 1, 32 * t, 32 * (t + 1))
-                if behind is not None:
-                    join(*behind[1:], quarter * t, quarter * (t + 1))
+                if behind is not None and t < 2:
+                    join(*behind[1:], t)
+                if behind is not None and t == 2:
+                    quantise_h(behind[0], behind[1], whole)
+                if n == 0 and t >= 2:
+                    gather_v2(t - 2)
             if b == 0:
-                gather_v2(half)
                 quantise_w1(half, 1)
-            if behind is not None:
-                quantise_h(behind[0], behind[1])
-                if behind[0] == (1, 0):
-                    score(0)
             h_bf = ring.tile([P, PACK * N], BF16, name="h_bf", align_bytes=64)
             behind = ((b, half), h_bf, apart, joint)
-        join(*behind[1:], 0, 4 * quarter)
-        quantise_h(behind[0], behind[1])
-        score(1)
+        scores = [held(tag, [P, S], F32) for tag in ("w1_raw10", "w1_raw01", "w1_raw11", "w4_raw")]
+        score(0, scores, [psum.tile([P, N], F32, name="x_ps", bufs=4) for g in range(S2 // P)], [whole])
+        for part in range(2):
+            join(*behind[1:], part)
+        for cols in halves:
+            quantise_h(behind[0], behind[1], cols)
+        score(1, scores, [psum.tile([P, N], F32, name="y_ps", bufs=4) for g in range(S2 // P)], halves)
 
         firsts, pairs = {}, {}
         groups = S2 // P
         for step in range(groups + 2):
             if step < groups:
-                firsts[step] = ring.tile([P, NP], F32, name="first", bufs=2)
+                firsts[step] = ring.tile([P, NP], F32, name="first", bufs=3)
                 nc.vector.tensor_copy(firsts[step][:], scores[step][:].indirect(p1[:]))
             g = step - 1
             if 0 <= g < groups:
-                pairs[g] = ring.tile([P, NP], F32, name="pair", bufs=2)
+                pairs[g] = ring.tile([P, NP], F32, name="pair", bufs=3)
                 nc.vector.tensor_tensor(pairs[g][:], scores[g][:].indirect(p2[:]), firsts[g][:], ALU.mult)
             g = step - 2
             if g >= 0:
-                result = ring.tile([P, NP], F32, name="result", bufs=3)
+                result = ring.tile([P, NP], F32, name="result", bufs=4)
                 nc.vector.tensor_tensor(out=result[:], in0=pairs[g][:], in1=typ_sb[:, g, :], op=ALU.subtract)
                 nc.sync.dma_start(out=out[P * g : P * (g + 1), :], in_=result[:])

@@ -1,6 +1,7 @@
 from contextlib import ExitStack
 
 import concourse.mybir as mybir
+from concourse.masks import make_identity
 
 K, H, T, S, T3, S2, NP = 1024, 1024, 4096, 1024, 2048, 512, 512
 FLOPS = 2 * (2 * K * H * S + H * S2 * S)
@@ -45,6 +46,9 @@ def tile_list_excerpt_pair_scores_kernel(
         w4_sc_raw = held("w4_sc_raw", [P, 2 * H], U8)
         for plane in (tab_sc, w4_sc_raw, tab2_sc):
             nc.vector.memset(plane[:].bitcast(I32), 0)
+
+        ident = held("ident", [P, P], F32)
+        make_identity(nc, ident[:])
 
         tab_w = [held(f"tab_w{a}", [P, T], I32) for a in range(2)]
         tab2_w = [held(f"tab2_w{a}", [P, T3], I32) for a in range(2)]
@@ -101,8 +105,8 @@ def tile_list_excerpt_pair_scores_kernel(
             if q0 == 0:
                 w1_bf[a, b] = held(f"w1_bf{a}", [P, PACK * PASS], BF16)
             nc.scalar.copy(
-                out=w1_bf[a, b][:].rearrange("p (t q j) -> p q j t", t=PACK, j=PACK)[:, q0:q1],
-                in_=w1_raw[a, b][:].rearrange("p j (q t) -> p q j t", t=PACK)[:, q0:q1],
+                out=w1_bf[a, b][:].rearrange("p (t q j) -> p q t j", t=PACK, j=PACK)[:, q0:q1],
+                in_=w1_raw[a, b][:].rearrange("p j (q t) -> p q t j", t=PACK)[:, q0:q1],
             )
 
         def quantise_w1(a, b):
@@ -114,9 +118,9 @@ def tile_list_excerpt_pair_scores_kernel(
         nc.scalar.dma_start(out=v_sc1[0 : P - 4, :].bitcast(I32), in_=v_sc[4:P, :].bitcast(I32))
 
         load_w1(0, 1)
+        load_w1(1, 1)
         load_words(tab2_w[0], tab2_words[0])
         load_words(tab2_w[1], tab2_words[1])
-        load_w1(1, 1)
         typ_sb = held("w1_raw00", [P, S2 // P, NP], F32)
         nc.sync.dma_start(out=typ_sb[:], in_=typ.rearrange("(g p) n -> p g n", p=P))
 
@@ -142,7 +146,7 @@ def tile_list_excerpt_pair_scores_kernel(
         h_c = {(b, half): held(f"h_c{b}{half}", [P, N], U32) for b in range(2) for half in range(2)}
         h_sc = {(b, half): held(f"h_sc{b}{half}", [P, N], U8) for b in range(2) for half in range(2)}
 
-        def readings(b, half, t, apart, joint):
+        def readings(b, half, t):
             x_ps = psum.tile([P, N], F32, name="x_ps", bufs=4)
             y_ps = psum.tile([P, N], F32, name="y_ps", bufs=4)
             cols = slice(N * half, N * (half + 1))
@@ -169,20 +173,27 @@ def tile_list_excerpt_pair_scores_kernel(
                 )
             x_sb = ring.tile([P, N], F32, name="x_sb", bufs=4)
             diff = ring.tile([P, N], F32, name="diff", bufs=3)
+            joint = ring.tile([P, N], F32, name="joint", bufs=4)
+            apart = ring.tile([P, N], F32, name="apart", bufs=4)
             nc.scalar.copy(out=x_sb[:], in_=x_ps[:])
             nc.vector.tensor_tensor(out=diff[:], in0=y_ps[:], in1=x_sb[:], op=ALU.subtract)
             nc.vector.scalar_tensor_tensor(
-                out=joint[:, t, :], in0=y_ps[:], scalar=gain[:, b, t : t + 1], in1=x_sb[:], op0=ALU.mult, op1=ALU.mult
+                out=joint[:], in0=y_ps[:], scalar=gain[:, b, t : t + 1], in1=x_sb[:], op0=ALU.mult, op1=ALU.mult
             )
-            nc.scalar.activation(out=apart[:, t, :], in_=diff[:], func=ACT.Abs)
+            nc.scalar.activation(out=apart[:], in_=diff[:], func=ACT.Abs)
+            return apart, joint
 
-        def join(h_bf, apart, joint, part):
-            pairs = slice(part * N // 4, (part + 1) * N // 4)
-            nc.vector.tensor_tensor(
-                out=h_bf[:].rearrange("p (c i t) -> p c t i", i=2, t=PACK)[:, pairs],
-                in0=apart[:].rearrange("p t (c i) -> p c t i", i=2)[:, pairs],
-                in1=joint[:].rearrange("p t (c i) -> p c t i", i=2)[:, pairs],
-                op=ALU.add,
+        def weave_on_scalar(h_bf, h_rows, cols):
+            nc.scalar.copy(
+                out=h_bf[:].rearrange("p (j t) -> p j t", t=PACK)[:, cols],
+                in_=h_rows[:].rearrange("p t j -> p j t")[:, cols],
+            )
+
+        def weave_on_vector(h_bf, h_rows, cols):
+            quads = slice(cols.start // 4, cols.stop // 4)
+            nc.vector.tensor_copy(
+                out=h_bf[:].rearrange("p (c i t) -> p c t i", i=4, t=PACK)[:, quads],
+                in_=h_rows[:].rearrange("p t (c i) -> p c t i", i=4)[:, quads],
             )
 
         def quantise_h(chunk, h_bf, cols):
@@ -215,31 +226,52 @@ def tile_list_excerpt_pair_scores_kernel(
         chunks = [(b, half) for b in range(2) for half in range(2)]
         whole = slice(0, N)
         halves = [slice(0, N // 2), slice(N // 2, N)]
-        behind = None
-        for n, (b, half) in enumerate(chunks):
-            apart = ring.tile([P, PACK, N], F32, name="apart")
-            joint = ring.tile([P, PACK, N], F32, name="joint")
-            for t in range(PACK):
-                readings(b, half, t, apart, joint)
-                if b == 0:
-                    round_w1(half, 1, 32 * t, 32 * (t + 1))
-                if behind is not None and t < 2:
-                    join(*behind[1:], t)
-                if behind is not None and t == 2:
-                    quantise_h(behind[0], behind[1], whole)
-                if n == 0 and t >= 2:
-                    gather_v2(t - 2)
-            if b == 0:
-                quantise_w1(half, 1)
-            h_bf = ring.tile([P, PACK * N], BF16, name="h_bf", align_bytes=64)
-            behind = ((b, half), h_bf, apart, joint)
+        steps = [(chunk, t) for chunk in chunks for t in range(PACK)]
+        terms, h_rows, h_bf = {}, {}, {}
+        typ_neg = held("typ_neg", [P, 2, NP], F32)
+        for n in range(len(steps) + 1):
+            if n < len(steps):
+                (b, half), t = steps[n]
+                terms[n] = readings(b, half, t)
+                if n < PACK:
+                    round_w1(n // 2, 1, 64 * (n % 2), 64 * (n % 2 + 1))
+                if n in (2, 4):
+                    quantise_w1(n // 2 - 1, 1)
+                if n in (2, 3):
+                    gather_v2(n - 2)
+            if n >= 1:
+                chunk, t = steps[n - 1]
+                if t == 0:
+                    h_rows[chunk] = ring.tile([P, PACK, N], BF16, name="h_rows")
+                apart, joint = terms[n - 1]
+                nc.vector.tensor_tensor(out=h_rows[chunk][:, t, :], in0=apart[:], in1=joint[:], op=ALU.add)
+                if t == PACK - 1:
+                    h_bf[chunk] = ring.tile([P, PACK * N], BF16, name="h_bf", align_bytes=64)
+            if PACK <= n < len(steps) and n % PACK < 2:
+                chunk = chunks[n // PACK - 1]
+                weave_on_scalar(h_bf[chunk], h_rows[chunk], halves[n % PACK])
+            if n in (2 * PACK + 2, 2 * PACK + 3):
+                g = n - 2 * PACK - 2
+                nc.scalar.activation(out=typ_neg[:, g, :], in_=typ_sb[:, g, :], func=ACT.Copy, scale=-1.0)
+            if PACK <= n < len(steps) and n % PACK == 2:
+                chunk = chunks[n // PACK - 1]
+                quantise_h(chunk, h_bf[chunk], whole)
+        last = chunks[-1]
+        weave_on_vector(h_bf[last], h_rows[last], halves[0])
+        weave_on_scalar(h_bf[last], h_rows[last], halves[1])
         scores = [held(tag, [P, S], F32) for tag in ("w1_raw10", "w1_raw01", "w1_raw11", "w4_raw")]
         score(0, scores, [psum.tile([P, N], F32, name="x_ps", bufs=4) for g in range(S2 // P)], [whole])
-        for part in range(2):
-            join(*behind[1:], part)
         for cols in halves:
-            quantise_h(behind[0], behind[1], cols)
+            quantise_h(last, h_bf[last], cols)
         score(1, scores, [psum.tile([P, N], F32, name="y_ps", bufs=4) for g in range(S2 // P)], halves)
+
+        def turn(bank, source, start, stop):
+            for k in range(NP // P):
+                cols = slice(P * k, P * (k + 1))
+                nc.tensor.matmul(
+                    bank[:, cols], source[:, cols], ident[:], is_transpose=True,
+                    start=start and k == 0, stop=stop and k == NP // P - 1,
+                )
 
         firsts, pairs = {}, {}
         groups = S2 // P
@@ -254,5 +286,15 @@ def tile_list_excerpt_pair_scores_kernel(
             g = step - 2
             if g >= 0:
                 result = ring.tile([P, NP], F32, name="result", bufs=4)
-                nc.vector.tensor_tensor(out=result[:], in0=pairs[g][:], in1=typ_sb[:, g, :], op=ALU.subtract)
+                if g < 2:
+                    turned_ps = psum.tile([P, NP], F32, name="x_ps", bufs=4)
+                    turn(turned_ps, typ_neg[:, g, :], True, False)
+                    turn(turned_ps, pairs[g][:], False, True)
+                    turned = ring.tile([P, NP], F32, name="x_sb", bufs=4)
+                    nc.scalar.copy(out=turned[:], in_=turned_ps[:])
+                    back_ps = psum.tile([P, NP], F32, name="x_ps", bufs=4)
+                    turn(back_ps, turned[:], True, True)
+                    nc.scalar.copy(out=result[:], in_=back_ps[:])
+                else:
+                    nc.vector.tensor_tensor(out=result[:], in0=pairs[g][:], in1=typ_sb[:, g, :], op=ALU.subtract)
                 nc.sync.dma_start(out=out[P * g : P * (g + 1), :], in_=result[:])

@@ -22,6 +22,10 @@ PACK = 4
 PASS = P * PACK
 N = 512
 LIST_COLS = N // 16
+GROUPS = S2 // P
+SECOND_PLANE = 16
+BANKS = 4
+TURNED_GROUPS = 2
 
 
 def tile_list_excerpt_pair_scores_kernel(
@@ -44,23 +48,17 @@ def tile_list_excerpt_pair_scores_kernel(
         tab_sc = held("tab_sc", [P, T], U8)
         tab2_sc = held("tab2_sc", [P, T3], U8)
         w4_sc_raw = held("w4_sc_raw", [P, 2 * H], U8)
-        for plane in (tab_sc, w4_sc_raw, tab2_sc):
-            nc.vector.memset(plane[:].bitcast(I32), 0)
+        for scale_tile in (tab_sc, w4_sc_raw, tab2_sc):
+            nc.vector.memset(scale_tile[:].bitcast(I32), 0)
 
         ident = held("ident", [P, P], F32)
         make_identity(nc, ident[:])
 
         tab_w = [held(f"tab_w{a}", [P, T], I32) for a in range(2)]
-        tab2_w = [held(f"tab2_w{a}", [P, T3], I32) for a in range(2)]
+        tab2_w = [held(f"tab2_w{b}", [P, T3], I32) for b in range(2)]
         w4_raw = held("w4_raw", [P, 2, 2 * H], U8)
         w1_raw = {}
         gain = held("gain", [P, 2, PACK], F32)
-
-        def load_scale_rows(window, scales):
-            for q in range(4):
-                nc.sync.dma_start(
-                    out=window[32 * q : 32 * q + 8, :].bitcast(I32), in_=scales[:, 4 * q : 4 * q + 4, :].bitcast(I32)
-                )
 
         def load_words(window, words):
             nc.sync.dma_start(out=window[:], in_=words.rearrange("p t i -> p (t i)").bitcast(I32))
@@ -70,21 +68,26 @@ def tile_list_excerpt_pair_scores_kernel(
             rows = w1[PASS * a : PASS * (a + 1), PASS * b : PASS * (b + 1)]
             nc.sync.dma_start(out=w1_raw[a, b][:], in_=rows.rearrange("(p j) c -> p j c", j=PACK))
 
-        for tile, entries in ((idx, offs), (idx2, offs2), (p1, pos1), (p2, pos2)):
-            nc.sync.dma_start(tile[:], entries)
+        for list_tile, entries in ((idx, offs), (idx2, offs2), (p1, pos1), (p2, pos2)):
+            nc.sync.dma_start(list_tile[:], entries)
         nc.sync.dma_start(out=gain[:], in_=gam.rearrange("(b p t) -> p b t", b=2, t=PACK))
         nc.sync.dma_start(out=w4_raw[:].bitcast(I32), in_=w4_words.rearrange("a p c -> p a c").bitcast(I32))
         load_w1(0, 0)
         load_w1(1, 0)
-        load_scale_rows(tab_sc, tab_scales)
+        tab_rows = tab_scales.bitcast(I32).rearrange("a (q s) t -> s q a t", s=4)
+        for s in range(4):
+            nc.sync.dma_start(out=tab_sc[s:P:SECOND_PLANE, :].bitcast(I32), in_=tab_rows[s])
         load_words(tab_w[0], tab_words[0])
         for q in range(4):
             nc.sync.dma_start(
-                out=w4_sc_raw[32 * q : 32 * q + 4, :].bitcast(I32).rearrange("r (a c) -> r a c", a=2),
-                in_=w4_scales[:, 4 * q : 4 * q + 4, :].bitcast(I32).rearrange("a r c -> r a c"),
+                out=w4_sc_raw[32 * q : 32 * q + 4, :].bitcast(I32).rearrange("s (a c) -> s a c", a=2),
+                in_=w4_scales[:, 4 * q : 4 * q + 4, :].bitcast(I32).rearrange("a s c -> s a c"),
             )
         load_words(tab_w[1], tab_words[1])
-        load_scale_rows(tab2_sc, tab2_scales)
+        for q in range(4):
+            nc.sync.dma_start(
+                out=tab2_sc[32 * q : 32 * q + 8, :].bitcast(I32), in_=tab2_scales[:, 4 * q : 4 * q + 4, :].bitcast(I32)
+            )
 
         w4_c = held("w4_c", [P, 4 * 2 * PASS], U8)
         nc.vector.tensor_copy(
@@ -115,13 +118,13 @@ def tile_list_excerpt_pair_scores_kernel(
         for a in range(2):
             round_w1(a, 0, 0, P)
             quantise_w1(a, 0)
-        nc.scalar.dma_start(out=v_sc1[0 : P - 4, :].bitcast(I32), in_=v_sc[4:P, :].bitcast(I32))
+        nc.scalar.dma_start(out=v_sc1[0 : P - SECOND_PLANE, :].bitcast(I32), in_=v_sc[SECOND_PLANE:P, :].bitcast(I32))
 
         load_w1(0, 1)
         load_w1(1, 1)
         load_words(tab2_w[0], tab2_words[0])
         load_words(tab2_w[1], tab2_words[1])
-        typ_sb = held("w1_raw00", [P, S2 // P, NP], F32)
+        typ_sb = held("w1_raw00", [P, GROUPS, NP], F32)
         nc.sync.dma_start(out=typ_sb[:], in_=typ.rearrange("(g p) n -> p g n", p=P))
 
         w4_sc = held("w4_sc", [P, 4 * PASS], U8)
@@ -147,8 +150,8 @@ def tile_list_excerpt_pair_scores_kernel(
         h_sc = {(b, half): held(f"h_sc{b}{half}", [P, N], U8) for b in range(2) for half in range(2)}
 
         def readings(b, half, t):
-            x_ps = psum.tile([P, N], F32, name="x_ps", bufs=4)
-            y_ps = psum.tile([P, N], F32, name="y_ps", bufs=4)
+            x_ps = psum.tile([P, N], F32, name="x_ps", bufs=BANKS)
+            y_ps = psum.tile([P, N], F32, name="y_ps", bufs=BANKS)
             cols = slice(N * half, N * (half + 1))
             for a in range(2):
                 nc.tensor.matmul_mx(
@@ -171,7 +174,7 @@ def tile_list_excerpt_pair_scores_kernel(
                     start=(a == 0),
                     stop=(a == 1),
                 )
-            x_sb = ring.tile([P, N], F32, name="x_sb", bufs=4)
+            x_sb = ring.tile([P, N], F32, name="x_sb", bufs=BANKS)
             diff = ring.tile([P, N], F32, name="diff", bufs=3)
             joint = ring.tile([P, N], F32, name="joint", bufs=4)
             apart = ring.tile([P, N], F32, name="apart", bufs=4)
@@ -183,24 +186,24 @@ def tile_list_excerpt_pair_scores_kernel(
             nc.scalar.activation(out=apart[:], in_=diff[:], func=ACT.Abs)
             return apart, joint
 
-        def weave_on_scalar(h_bf, h_rows, cols):
+        def weave_on_scalar(woven, rows, cols):
             nc.scalar.copy(
-                out=h_bf[:].rearrange("p (j t) -> p j t", t=PACK)[:, cols],
-                in_=h_rows[:].rearrange("p t j -> p j t")[:, cols],
+                out=woven[:].rearrange("p (j t) -> p j t", t=PACK)[:, cols],
+                in_=rows[:].rearrange("p t j -> p j t")[:, cols],
             )
 
-        def weave_on_vector(h_bf, h_rows, cols):
+        def weave_on_vector(woven, rows, cols):
             quads = slice(cols.start // 4, cols.stop // 4)
             nc.vector.tensor_copy(
-                out=h_bf[:].rearrange("p (c i t) -> p c t i", i=4, t=PACK)[:, quads],
-                in_=h_rows[:].rearrange("p t (c i) -> p c t i", i=4)[:, quads],
+                out=woven[:].rearrange("p (c i t) -> p c t i", i=4, t=PACK)[:, quads],
+                in_=rows[:].rearrange("p t (c i) -> p c t i", i=4)[:, quads],
             )
 
-        def quantise_h(chunk, h_bf, cols):
+        def quantise_h(chunk, woven, cols):
             nc.vector.quantize_mx(
                 out=h_c[chunk][:, cols].bitcast(FP8X4),
                 scales=h_sc[chunk][:, cols],
-                in_=h_bf[:, PACK * cols.start : PACK * cols.stop],
+                in_=woven[:, PACK * cols.start : PACK * cols.stop],
             )
 
         def score_pass(bank, g, b, half, cols, start, stop):
@@ -214,27 +217,24 @@ def tile_list_excerpt_pair_scores_kernel(
                 stop=stop,
             )
 
-        def score(half, scores, banks, last_parts):
+        def score(half, banks, parts):
             for g, bank in enumerate(banks):
                 score_pass(bank, g, 0, half, slice(0, N), True, False)
-            for cols in last_parts:
+            for cols in parts:
                 for g, bank in enumerate(banks):
                     score_pass(bank, g, 1, half, cols, False, cols.stop == N)
-            for g, bank in enumerate(banks):
-                nc.scalar.copy(out=scores[g][:, N * half : N * (half + 1)], in_=bank[:])
 
         chunks = [(b, half) for b in range(2) for half in range(2)]
         whole = slice(0, N)
-        halves = [slice(0, N // 2), slice(N // 2, N)]
+        parts = [slice(0, N // 2), slice(N // 2, N)]
         steps = [(chunk, t) for chunk in chunks for t in range(PACK)]
         terms, h_rows, h_bf = {}, {}, {}
-        typ_neg = held("typ_neg", [P, 2, NP], F32)
         for n in range(len(steps) + 1):
             if n < len(steps):
                 (b, half), t = steps[n]
                 terms[n] = readings(b, half, t)
                 if n < PACK:
-                    round_w1(n // 2, 1, 64 * (n % 2), 64 * (n % 2 + 1))
+                    round_w1(n // 2, 1, (P // 2) * (n % 2), (P // 2) * (n % 2 + 1))
                 if n in (2, 4):
                     quantise_w1(n // 2 - 1, 1)
                 if n in (2, 3):
@@ -247,52 +247,60 @@ def tile_list_excerpt_pair_scores_kernel(
                 nc.vector.tensor_tensor(out=h_rows[chunk][:, t, :], in0=apart[:], in1=joint[:], op=ALU.add)
                 if t == PACK - 1:
                     h_bf[chunk] = ring.tile([P, PACK * N], BF16, name="h_bf", align_bytes=64)
-            if PACK <= n < len(steps) and n % PACK < 2:
+            if PACK <= n < len(steps) and n % PACK < len(parts):
                 chunk = chunks[n // PACK - 1]
-                weave_on_scalar(h_bf[chunk], h_rows[chunk], halves[n % PACK])
-            if n in (2 * PACK + 2, 2 * PACK + 3):
-                g = n - 2 * PACK - 2
-                nc.scalar.activation(out=typ_neg[:, g, :], in_=typ_sb[:, g, :], func=ACT.Copy, scale=-1.0)
-            if PACK <= n < len(steps) and n % PACK == 2:
+                weave_on_scalar(h_bf[chunk], h_rows[chunk], parts[n % PACK])
+            if PACK <= n < len(steps) and n % PACK == len(parts):
                 chunk = chunks[n // PACK - 1]
                 quantise_h(chunk, h_bf[chunk], whole)
+
         last = chunks[-1]
-        weave_on_vector(h_bf[last], h_rows[last], halves[0])
-        weave_on_scalar(h_bf[last], h_rows[last], halves[1])
-        scores = [held(tag, [P, S], F32) for tag in ("w1_raw10", "w1_raw01", "w1_raw11", "w4_raw")]
-        score(0, scores, [psum.tile([P, N], F32, name="x_ps", bufs=4) for g in range(S2 // P)], [whole])
-        for cols in halves:
+        weave_on_vector(h_bf[last], h_rows[last], parts[0])
+        weave_on_scalar(h_bf[last], h_rows[last], parts[1])
+        scores = [held(name, [P, S], F32) for name in ("w1_raw10", "w1_raw01", "w1_raw11", "w4_raw")]
+        banks = [[psum.tile([P, N], F32, name=name, bufs=BANKS) for g in range(GROUPS)] for name in ("x_ps", "y_ps")]
+        score(0, banks[0], [whole])
+        for cols in parts:
             quantise_h(last, h_bf[last], cols)
-        score(1, scores, [psum.tile([P, N], F32, name="y_ps", bufs=4) for g in range(S2 // P)], halves)
+        score(1, banks[1], parts)
+        for g in range(GROUPS):
+            for half in range(2):
+                nc.scalar.copy(out=scores[g][:, N * half : N * (half + 1)], in_=banks[half][g][:])
+        typ_neg = held("typ_neg", [P, TURNED_GROUPS, NP], F32)
+        for g in range(TURNED_GROUPS):
+            nc.scalar.activation(out=typ_neg[:, g, :], in_=typ_sb[:, g, :], func=ACT.Copy, scale=-1.0)
 
         def turn(bank, source, start, stop):
             for k in range(NP // P):
                 cols = slice(P * k, P * (k + 1))
                 nc.tensor.matmul(
-                    bank[:, cols], source[:, cols], ident[:], is_transpose=True,
-                    start=start and k == 0, stop=stop and k == NP // P - 1,
+                    bank[:, cols],
+                    source[:, cols],
+                    ident[:],
+                    is_transpose=True,
+                    start=start and k == 0,
+                    stop=stop and k == NP // P - 1,
                 )
 
         firsts, pairs = {}, {}
-        groups = S2 // P
-        for step in range(groups + 2):
-            if step < groups:
+        for step in range(GROUPS + 2):
+            if step < GROUPS:
                 firsts[step] = ring.tile([P, NP], F32, name="first", bufs=3)
                 nc.vector.tensor_copy(firsts[step][:], scores[step][:].indirect(p1[:]))
             g = step - 1
-            if 0 <= g < groups:
+            if 0 <= g < GROUPS:
                 pairs[g] = ring.tile([P, NP], F32, name="pair", bufs=3)
                 nc.vector.tensor_tensor(pairs[g][:], scores[g][:].indirect(p2[:]), firsts[g][:], ALU.mult)
             g = step - 2
             if g >= 0:
-                result = ring.tile([P, NP], F32, name="result", bufs=4)
-                if g < 2:
-                    turned_ps = psum.tile([P, NP], F32, name="x_ps", bufs=4)
+                result = ring.tile([P, NP], F32, name="result", bufs=GROUPS)
+                if g < TURNED_GROUPS:
+                    turned_ps = psum.tile([P, NP], F32, name="x_ps", bufs=BANKS)
                     turn(turned_ps, typ_neg[:, g, :], True, False)
                     turn(turned_ps, pairs[g][:], False, True)
-                    turned = ring.tile([P, NP], F32, name="x_sb", bufs=4)
+                    turned = ring.tile([P, NP], F32, name="x_sb", bufs=BANKS)
                     nc.scalar.copy(out=turned[:], in_=turned_ps[:])
-                    back_ps = psum.tile([P, NP], F32, name="x_ps", bufs=4)
+                    back_ps = psum.tile([P, NP], F32, name="x_ps", bufs=BANKS)
                     turn(back_ps, turned[:], True, True)
                     nc.scalar.copy(out=result[:], in_=back_ps[:])
                 else:

from contextlib import ExitStack

import concourse.mybir as mybir
from concourse.masks import make_identity

K, H, T, S, T3, S2, NP = 1024, 1024, 4096, 1024, 2048, 512, 512
FLOPS = 2 * (2 * K * H * S + H * S2 * S)

F32 = mybir.dt.float32
BF16 = mybir.dt.bfloat16
I32 = mybir.dt.int32
U32 = mybir.dt.uint32
U16 = mybir.dt.uint16
U8 = mybir.dt.uint8
FP8X4 = mybir.dt.float8_e4m3fn_x4
FP4X4 = mybir.dt.float4_e2m1fn_x4
ALU = mybir.AluOpType
ACT = mybir.ActivationFunctionType

P = 128
PACK = 4
PASS = P * PACK
N = 512
LIST_COLS = N // 16
GROUPS = S2 // P
SECOND_PLANE = 16
BANKS = 4
TURNED_GROUPS = 2


def tile_list_excerpt_pair_scores_kernel(
    tc, tab_words, tab_scales, offs, w1, w4_words, w4_scales, gam, tab2_words, tab2_scales, offs2, pos1, pos2, typ, out
):
    nc = tc.nc
    with ExitStack() as ctx:
        keep = ctx.enter_context(tc.tile_pool(name="keep", bufs=1))
        ring = ctx.enter_context(tc.tile_pool(name="ring", bufs=2))
        psum = ctx.enter_context(tc.psum_pool(name="psum", bufs=1))

        def held(name, shape, dtype):
            return keep.tile(shape, dtype, name=name, align_bytes=64)

        idx = held("idx", [P, S // 16], U16)
        idx2 = held("idx2", [P, S2 // 16], U16)
        p1 = held("p1", [P, NP // 16], U16)
        p2 = held("p2", [P, NP // 16], U16)

        tab_sc = held("tab_sc", [P, T], U8)
        tab2_sc = held("tab2_sc", [P, T3], U8)
        w4_sc_raw = held("w4_sc_raw", [P, 2 * H], U8)
        for scale_tile in (tab_sc, w4_sc_raw, tab2_sc):
            nc.vector.memset(scale_tile[:].bitcast(I32), 0)

        ident = held("ident", [P, P], F32)
        make_identity(nc, ident[:])

        tab_w = [held(f"tab_w{a}", [P, T], I32) for a in range(2)]
        tab2_w = [held(f"tab2_w{b}", [P, T3], I32) for b in range(2)]
        w4_raw = held("w4_raw", [P, 2, 2 * H], U8)
        w1_raw = {}
        gain = held("gain", [P, 2, PACK], F32)

        def load_words(window, words):
            nc.sync.dma_start(out=window[:], in_=words.rearrange("p t i -> p (t i)").bitcast(I32))

        def load_w1(a, b):
            w1_raw[a, b] = held(f"w1_raw{a}{b}", [P, PACK, PASS], F32)
            rows = w1[PASS * a : PASS * (a + 1), PASS * b : PASS * (b + 1)]
            nc.sync.dma_start(out=w1_raw[a, b][:], in_=rows.rearrange("(p j) c -> p j c", j=PACK))

        for list_tile, entries in ((idx, offs), (idx2, offs2), (p1, pos1), (p2, pos2)):
            nc.sync.dma_start(list_tile[:], entries)
        nc.sync.dma_start(out=gain[:], in_=gam.rearrange("(b p t) -> p b t", b=2, t=PACK))
        nc.sync.dma_start(out=w4_raw[:].bitcast(I32), in_=w4_words.rearrange("a p c -> p a c").bitcast(I32))
        load_w1(0, 0)
        load_w1(1, 0)
        tab_rows = tab_scales.bitcast(I32).rearrange("a (q s) t -> s q a t", s=4)
        for s in range(4):
            nc.sync.dma_start(out=tab_sc[s:P:SECOND_PLANE, :].bitcast(I32), in_=tab_rows[s])
        load_words(tab_w[0], tab_words[0])
        for q in range(4):
            nc.sync.dma_start(
                out=w4_sc_raw[32 * q : 32 * q + 4, :].bitcast(I32).rearrange("s (a c) -> s a c", a=2),
                in_=w4_scales[:, 4 * q : 4 * q + 4, :].bitcast(I32).rearrange("a s c -> s a c"),
            )
        load_words(tab_w[1], tab_words[1])
        for q in range(4):
            nc.sync.dma_start(
                out=tab2_sc[32 * q : 32 * q + 8, :].bitcast(I32), in_=tab2_scales[:, 4 * q : 4 * q + 4, :].bitcast(I32)
            )

        w4_c = held("w4_c", [P, 4 * 2 * PASS], U8)
        nc.vector.tensor_copy(
            out=w4_c[:].bitcast(U16).rearrange("p (g t q) -> p g t q", g=4, t=PACK),
            in_=w4_raw[:].rearrange("p a c -> p (a c)").bitcast(U16).rearrange("p (g q t) -> p g t q", g=4, t=PACK),
        )

        v_sc = held("v_sc", [P, S], U8)
        v_sc1 = held("v_sc1", [P, S], U8)
        nc.vector.tensor_copy(v_sc[:], tab_sc[:].indirect(idx[:]))
        v_planes = [v_sc, v_sc1]

        w1_bf = {}
        w1_c = {(a, b): held(f"w1_c{a}{b}", [P, PASS], U32) for a in range(2) for b in range(2)}
        w1_sc = {(a, b): held(f"w1_sc{a}{b}", [P, PASS], U8) for a in range(2) for b in range(2)}

        def round_w1(a, b, q0, q1):
            if q0 == 0:
                w1_bf[a, b] = held(f"w1_bf{a}", [P, PACK * PASS], BF16)
            nc.scalar.copy(
                out=w1_bf[a, b][:].rearrange("p (t q j) -> p q t j", t=PACK, j=PACK)[:, q0:q1],
                in_=w1_raw[a, b][:].rearrange("p j (q t) -> p q t j", t=PACK)[:, q0:q1],
            )

        def quantise_w1(a, b):
            nc.vector.quantize_mx(out=w1_c[a, b][:].bitcast(FP8X4), scales=w1_sc[a, b][:], in_=w1_bf[a, b][:])

        for a in range(2):
            round_w1(a, 0, 0, P)
            quantise_w1(a, 0)
        nc.scalar.dma_start(out=v_sc1[0 : P - SECOND_PLANE, :].bitcast(I32), in_=v_sc[SECOND_PLANE:P, :].bitcast(I32))

        load_w1(0, 1)
        load_w1(1, 1)
        load_words(tab2_w[0], tab2_words[0])
        load_words(tab2_w[1], tab2_words[1])
        typ_sb = held("w1_raw00", [P, GROUPS, NP], F32)
        nc.sync.dma_start(out=typ_sb[:], in_=typ.rearrange("(g p) n -> p g n", p=P))

        w4_sc = held("w4_sc", [P, 4 * PASS], U8)
        v_w = {(a, half): held(f"v_w{a}{half}", [P, N], U32) for a in range(2) for half in range(2)}
        for a in range(2):
            for half in range(2):
                picks = idx[:, LIST_COLS * half : LIST_COLS * (half + 1)]
                nc.vector.tensor_copy(v_w[a, half][:], tab_w[a][:].bitcast(U32).indirect(picks))
            if a == 0:
                nc.vector.tensor_copy(
                    out=w4_sc[:].rearrange("p (g t q) -> p g t q", g=4, t=PACK),
                    in_=w4_sc_raw[:].rearrange("p (g q t) -> p g t q", g=4, t=PACK),
                )

        v2_sc = held("v2_sc", [P, S2], U8)
        nc.vector.tensor_copy(v2_sc[:], tab2_sc[:].indirect(idx2[:]))
        v2_w = [held(f"v2_w{b}", [P, S2], U32) for b in range(2)]

        def gather_v2(b):
            nc.vector.tensor_copy(v2_w[b][:], tab2_w[b][:].bitcast(U32).indirect(idx2[:]))

        h_c = {(b, half): held(f"h_c{b}{half}", [P, N], U32) for b in range(2) for half in range(2)}
        h_sc = {(b, half): held(f"h_sc{b}{half}", [P, N], U8) for b in range(2) for half in range(2)}

        def readings(b, half, t):
            x_ps = psum.tile([P, N], F32, name="x_ps", bufs=BANKS)
            y_ps = psum.tile([P, N], F32, name="y_ps", bufs=BANKS)
            cols = slice(N * half, N * (half + 1))
            for a in range(2):
                nc.tensor.matmul_mx(
                    out=x_ps[:],
                    lhsT=w1_c[a, b][:, P * t : P * (t + 1)].bitcast(FP8X4),
                    lhsT_scale=w1_sc[a, b][:, P * t : P * (t + 1)],
                    rhs=v_w[a, half][:].bitcast(FP8X4),
                    rhs_scale=v_planes[a][:, cols],
                    start=(a == 0),
                    stop=(a == 1),
                )
            for a in range(2):
                first = PASS * (2 * a + b) + P * t
                nc.tensor.matmul_mx(
                    out=y_ps[:],
                    lhsT=w4_c[:, 2 * first : 2 * (first + P)].bitcast(FP4X4),
                    lhsT_scale=w4_sc[:, first : first + P],
                    rhs=v_w[a, half][:].bitcast(FP8X4),
                    rhs_scale=v_planes[a][:, cols],
                    start=(a == 0),
                    stop=(a == 1),
                )
            x_sb = ring.tile([P, N], F32, name="x_sb", bufs=BANKS)
            diff = ring.tile([P, N], F32, name="diff", bufs=3)
            joint = ring.tile([P, N], F32, name="joint", bufs=4)
            apart = ring.tile([P, N], F32, name="apart", bufs=4)
            nc.scalar.copy(out=x_sb[:], in_=x_ps[:])
            nc.vector.tensor_tensor(out=diff[:], in0=y_ps[:], in1=x_sb[:], op=ALU.subtract)
            nc.vector.scalar_tensor_tensor(
                out=joint[:], in0=y_ps[:], scalar=gain[:, b, t : t + 1], in1=x_sb[:], op0=ALU.mult, op1=ALU.mult
            )
            nc.scalar.activation(out=apart[:], in_=diff[:], func=ACT.Abs)
            return apart, joint

        def weave_on_scalar(woven, rows, cols):
            nc.scalar.copy(
                out=woven[:].rearrange("p (j t) -> p j t", t=PACK)[:, cols],
                in_=rows[:].rearrange("p t j -> p j t")[:, cols],
            )

        def weave_on_vector(woven, rows, cols):
            quads = slice(cols.start // 4, cols.stop // 4)
            nc.vector.tensor_copy(
                out=woven[:].rearrange("p (c i t) -> p c t i", i=4, t=PACK)[:, quads],
                in_=rows[:].rearrange("p t (c i) -> p c t i", i=4)[:, quads],
            )

        def quantise_h(chunk, woven, cols):
            nc.vector.quantize_mx(
                out=h_c[chunk][:, cols].bitcast(FP8X4),
                scales=h_sc[chunk][:, cols],
                in_=woven[:, PACK * cols.start : PACK * cols.stop],
            )

        def score_pass(bank, g, b, half, cols, start, stop):
            nc.tensor.matmul_mx(
                out=bank[:, cols],
                lhsT=v2_w[b][:, P * g : P * (g + 1)].bitcast(FP8X4),
                lhsT_scale=v2_sc[4 * b : P, P * g : P * (g + 1)],
                rhs=h_c[b, half][:, cols].bitcast(FP8X4),
                rhs_scale=h_sc[b, half][:, cols],
                start=start,
                stop=stop,
            )

        def score(half, banks, parts):
            for g, bank in enumerate(banks):
                score_pass(bank, g, 0, half, slice(0, N), True, False)
            for cols in parts:
                for g, bank in enumerate(banks):
                    score_pass(bank, g, 1, half, cols, False, cols.stop == N)

        chunks = [(b, half) for b in range(2) for half in range(2)]
        whole = slice(0, N)
        parts = [slice(0, N // 2), slice(N // 2, N)]
        steps = [(chunk, t) for chunk in chunks for t in range(PACK)]
        terms, h_rows, h_bf = {}, {}, {}
        for n in range(len(steps) + 1):
            if n < len(steps):
                (b, half), t = steps[n]
                terms[n] = readings(b, half, t)
                if n < PACK:
                    round_w1(n // 2, 1, (P // 2) * (n % 2), (P // 2) * (n % 2 + 1))
                if n in (2, 4):
                    quantise_w1(n // 2 - 1, 1)
                if n in (2, 3):
                    gather_v2(n - 2)
            if n >= 1:
                chunk, t = steps[n - 1]
                if t == 0:
                    h_rows[chunk] = ring.tile([P, PACK, N], BF16, name="h_rows")
                apart, joint = terms[n - 1]
                nc.vector.tensor_tensor(out=h_rows[chunk][:, t, :], in0=apart[:], in1=joint[:], op=ALU.add)
                if t == PACK - 1:
                    h_bf[chunk] = ring.tile([P, PACK * N], BF16, name="h_bf", align_bytes=64)
            if PACK <= n < len(steps) and n % PACK < len(parts):
                chunk = chunks[n // PACK - 1]
                weave_on_scalar(h_bf[chunk], h_rows[chunk], parts[n % PACK])
            if PACK <= n < len(steps) and n % PACK == len(parts):
                chunk = chunks[n // PACK - 1]
                quantise_h(chunk, h_bf[chunk], whole)

        last = chunks[-1]
        weave_on_vector(h_bf[last], h_rows[last], parts[0])
        weave_on_scalar(h_bf[last], h_rows[last], parts[1])
        scores = [held(name, [P, S], F32) for name in ("w1_raw10", "w1_raw01", "w1_raw11", "w4_raw")]
        banks = [[psum.tile([P, N], F32, name=name, bufs=BANKS) for g in range(GROUPS)] for name in ("x_ps", "y_ps")]
        score(0, banks[0], [whole])
        for cols in parts:
            quantise_h(last, h_bf[last], cols)
        score(1, banks[1], parts)
        for g in range(GROUPS):
            for half in range(2):
                nc.scalar.copy(out=scores[g][:, N * half : N * (half + 1)], in_=banks[half][g][:])
        typ_neg = held("typ_neg", [P, TURNED_GROUPS, NP], F32)
        for g in range(TURNED_GROUPS):
            nc.scalar.activation(out=typ_neg[:, g, :], in_=typ_sb[:, g, :], func=ACT.Copy, scale=-1.0)

        def turn(bank, source, start, stop):
            for k in range(NP // P):
                cols = slice(P * k, P * (k + 1))
                nc.tensor.matmul(
                    bank[:, cols],
                    source[:, cols],
                    ident[:],
                    is_transpose=True,
                    start=start and k == 0,
                    stop=stop and k == NP // P - 1,
                )

        firsts, pairs = {}, {}
        for step in range(GROUPS + 2):
            if step < GROUPS:
                firsts[step] = ring.tile([P, NP], F32, name="first", bufs=3)
                nc.vector.tensor_copy(firsts[step][:], scores[step][:].indirect(p1[:]))
            g = step - 1
            if 0 <= g < GROUPS:
                pairs[g] = ring.tile([P, NP], F32, name="pair", bufs=3)
                nc.vector.tensor_tensor(pairs[g][:], scores[g][:].indirect(p2[:]), firsts[g][:], ALU.mult)
            g = step - 2
            if g >= 0:
                result = ring.tile([P, NP], F32, name="result", bufs=GROUPS)
                if g < TURNED_GROUPS:
                    turned_ps = psum.tile([P, NP], F32, name="x_ps", bufs=BANKS)
                    turn(turned_ps, typ_neg[:, g, :], True, False)
                    turn(turned_ps, pairs[g][:], False, True)
                    turned = ring.tile([P, NP], F32, name="x_sb", bufs=BANKS)
                    nc.scalar.copy(out=turned[:], in_=turned_ps[:])
                    back_ps = psum.tile([P, NP], F32, name="x_ps", bufs=BANKS)
                    turn(back_ps, turned[:], True, True)
                    nc.scalar.copy(out=result[:], in_=back_ps[:])
                else:
                    nc.vector.tensor_tensor(out=result[:], in0=pairs[g][:], in1=typ_sb[:, g, :], op=ALU.subtract)
                nc.sync.dma_start(out=out[P * g : P * (g + 1), :], in_=result[:])
